import numpy as np
import ml_dtypes


def mxq(x, axis, fmt="e4m3"):
    dtype, down = {"e4m3": (ml_dtypes.float8_e4m3fn, 7), "e5m2": (ml_dtypes.float8_e5m2, 14)}[fmt]
    v = np.moveaxis(np.asarray(x, np.float32).astype(ml_dtypes.bfloat16).astype(np.float64), axis, -1)
    blocks = v.reshape(v.shape[:-1] + (-1, 32))
    amax = np.abs(blocks).max(-1, keepdims=True)
    byte = np.maximum(np.where(amax > 0, np.frexp(amax)[1] - 1 + 127, 0) - down, 1)
    scale = np.exp2(byte - 127.0)
    codes = (blocks / scale).astype(np.float32).astype(dtype).astype(np.float64)
    return np.moveaxis((codes * scale).reshape(v.shape), -1, axis)


WIDE = False


def mx_kscale(k):
    if not WIDE:
        return np.ones(k)
    levels = np.array([10, -10, 5, -5, 0])
    if k % 512:
        return np.exp2(np.random.permutation(np.resize(levels, k // 32))).repeat(32)
    a = np.empty((k // 512, 16))
    for p in range(k // 512):
        a[p, :8] = np.random.permutation(np.resize(levels, 8))
        for g in range(8):
            far = levels[np.abs(levels - a[p, g]) >= 10]
            a[p, g + 8] = far[np.random.randint(len(far))]
    return np.exp2(a.ravel()).repeat(32)


def f64(x):
    return np.asarray(x).astype(np.float64)


def striped(idx):
    return np.tile(idx.reshape(-1, 16).T, (8, 1)).astype(np.uint16)


def unstriped(offs):
    return offs[:16].T.reshape(-1).astype(np.int64)


def pack_weight(w):
    k, n = w.shape
    w = f64(np.asarray(w, np.float32).astype(ml_dtypes.bfloat16)).reshape(k // 32, 32, n)
    amax = np.abs(w).max(1)
    byte = np.clip(np.where(amax > 0, np.frexp(amax)[1] - 1 + 127 - 7, 1), 1, 254)
    scaled = (w * np.exp2(127.0 - byte)[:, None, :]).reshape(k, n).astype(np.float32)
    words = np.ascontiguousarray(scaled.reshape(k // 512, 128, 4, n).transpose(0, 1, 3, 2)).astype(ml_dtypes.float8_e4m3fn).view(np.uint8)
    return words, np.ascontiguousarray(byte.astype(np.uint8).reshape(k // 512, 16, n))


def unpack_weight(words, scales):
    g, p, n, _ = words.shape
    vals = np.ascontiguousarray(words).view(ml_dtypes.float8_e4m3fn).astype(np.float64) * np.repeat(np.exp2(scales.astype(np.float64) - 127.0), 8, axis=1)[..., None]
    return vals.transpose(0, 1, 3, 2).reshape(g * 512, n)


def planes(y):
    n, m = y.shape
    v = y.astype(np.float32).astype(ml_dtypes.bfloat16).astype(np.float64).reshape(n // 32, 32, m)
    top = np.abs(v).max(1)
    byte = np.clip(np.where(top > 0, np.frexp(top)[1] - 1 + 127 - 7, 1), 1, 254)
    codes = (v * np.exp2(127.0 - byte)[:, None, :]).reshape(n, m).astype(np.float32).astype(ml_dtypes.float8_e4m3fn).view(np.uint8)
    words = codes.reshape(n // 512, 128, 4, m).transpose(0, 1, 3, 2)
    return np.ascontiguousarray(words), np.ascontiguousarray(byte.astype(np.uint8).reshape(n // 512, 16, m))


def gelu(v):
    return 0.5 * v * (1.0 + np.tanh(np.sqrt(2.0 / np.pi) * (v + 0.044715 * v**3)))


K, T, S, J = 1024, 4096, 1024, 512


def setup_inputs():
    n = np.random.standard_normal
    s = mx_kscale(K)[:, None]
    packed_xT = pack_weight(n((K, T)) * s)
    packed_eT = pack_weight(n((K, T)) * s)
    return {
        "x_words": packed_xT[0],
        "x_scales": packed_xT[1],
        "e_words": packed_eT[0],
        "e_scales": packed_eT[1],
        "hT": (n((K, J)) / np.sqrt(K) / s).astype(np.float32),
        "offs": striped(np.random.permutation(T)[:S]),
    }


def reference(x_words, x_scales, e_words, e_scales, hT, offs):
    xq = unpack_weight(x_words, x_scales)[:, unstriped(offs)]
    hTq = mxq(f64(hT), 0, "e4m3")
    y = xq.T @ hTq
    e_offs = unpack_weight(e_words, e_scales)[:, unstriped(offs)]
    e = e_offs.T @ hTq
    out_0 = gelu(y) * e
    return (out_0,) + planes(out_0)

@@ -1,0 +1,157 @@
+from contextlib import ExitStack
+
+import concourse.mybir as mybir
+
+K, T, S, J = 1024, 4096, 1024, 512
+FLOPS = 2 * 2 * K * S * J
+
+F32 = mybir.dt.float32
+BF16 = mybir.dt.bfloat16
+I32 = mybir.dt.int32
+U32 = mybir.dt.uint32
+U16 = mybir.dt.uint16
+U8 = mybir.dt.uint8
+FP8X4 = mybir.dt.float8_e4m3fn_x4
+GELU = mybir.ActivationFunctionType.Gelu_apprx_tanh
+MULT = mybir.AluOpType.mult
+
+P = 128
+PACK = 4
+SPAN = P * PACK
+PASSES = K // SPAN
+GROUPS = S // SPAN
+QUADS = 4
+HALVES = 2
+HALF = J // HALVES
+
+
+def tile_picked_zdejag_gelu_po_kernel(tc, x_words, x_scales, e_words, e_scales, hT, offs, out_0, out_1, out_2):
+    nc = tc.nc
+    with ExitStack() as ctx:
+        keep = ctx.enter_context(tc.tile_pool(name="keep", bufs=1))
+        psum = ctx.enter_context(tc.psum_pool(name="psum", bufs=1))
+
+        offsets = keep.tile([P, S // 16], U16, name="offsets")
+        scale_row0 = {"x": 0, "e": PASSES * 4}
+        word_src = {"x": x_words, "e": e_words}
+        scale_src = {"x": x_scales, "e": e_scales}
+        word_win, scale_win = {}, {}
+        for tab in "xe":
+            scale_win[tab] = keep.tile([P, T], U8, name="scale_win_" + tab, align_bytes=64)
+            nc.vector.memset(scale_win[tab][:].bitcast(I32), 0)
+
+        def load_words(tab, o):
+            win = keep.tile([P, T], U32, name="word_win_%s%d" % (tab, o), align_bytes=64)
+            nc.sync.dma_start(out=win[:].bitcast(I32), in_=word_src[tab][o].rearrange("p n t -> p (n t)").bitcast(I32))
+            word_win[tab, o] = win
+
+        def load_scales(tab):
+            for q in range(QUADS):
+                r0 = 32 * q + scale_row0[tab]
+                nc.sync.dma_start(out=scale_win[tab][r0 : r0 + 4 * PASSES, :].bitcast(I32),
+                                  in_=scale_src[tab][:, 4 * q : 4 * q + 4, :].bitcast(I32))
+
+        h_raw = {}
+
+        def load_h(o):
+            h_raw[o] = keep.tile([P, PACK, J], F32, name="h_raw%d" % o)
+            nc.sync.dma_start(out=h_raw[o][:], in_=hT[o * SPAN : (o + 1) * SPAN, :].rearrange("(p t) j -> p t j", t=PACK))
+
+        load_words("x", 0)
+        nc.sync.dma_start(offsets[:], offs)
+        load_scales("x")
+        load_h(0)
+        load_h(1)
+        load_scales("e")
+        load_words("x", 1)
+        load_words("e", 0)
+        load_words("e", 1)
+
+        def interleave(dst, src):
+            nc.scalar.copy(out=dst[:].rearrange("p (c i) t -> p c t i", i=4), in_=src[:].rearrange("p t (c i) -> p c t i", i=4))
+
+        words, scales, h_codes, h_scales = {}, {}, {}, {}
+
+        def gather_words(tab, o, g):
+            picked = keep.tile([P, SPAN], U32, name="words_%s%d%d" % (tab, o, g), align_bytes=64)
+            cols = slice(g * SPAN // 16, (g + 1) * SPAN // 16)
+            nc.vector.tensor_copy(picked[:].rearrange("p (t s) -> p s t", t=PACK), word_win[tab, o][:].indirect(offsets[:, cols]))
+            words[tab, o, g] = picked
+
+        def gather_scales(tab):
+            picked = keep.tile([P, S], U8, name="picked_scales_" + tab, align_bytes=64)
+            nc.vector.tensor_copy(picked[:], scale_win[tab][:].indirect(offsets[:]))
+            return picked
+
+        def deal_scales(tab, picked):
+            dealt = keep.tile([P, S], U8, name="scales_" + tab, align_bytes=64)
+            nc.vector.tensor_copy(dealt[:].rearrange("p (g t s) -> p g t s", g=GROUPS, t=PACK),
+                                  picked[:].rearrange("p (g s t) -> p g t s", g=GROUPS, t=PACK))
+            scales[tab] = dealt
+
+        def quantize_h(o):
+            rounded = keep.tile([P, J, PACK], BF16, name="h_rounded%d" % o, align_bytes=64)
+            interleave(rounded, h_raw[o])
+            h_codes[o] = keep.tile([P, J], U32, name="h_codes%d" % o, align_bytes=64)
+            h_scales[o] = keep.tile([P, J], U8, name="h_scales%d" % o, align_bytes=64)
+            nc.vector.quantize_mx(out=h_codes[o][:].bitcast(FP8X4), scales=h_scales[o][:], in_=rounded[:].rearrange("p j t -> p (j t)"))
+
+        acc = {}
+
+        def products(tab, o, g):
+            for t in range(PACK):
+                if o == 0:
+                    acc[tab, g, t] = psum.tile([P, J], F32, name="acc_%s%d%d" % (tab, g, t), tag="bank%d%d" % (g, t))
+                k0 = scale_row0[tab] + 4 * o
+                nc.tensor.matmul_mx(
+                    out=acc[tab, g, t][:],
+                    lhsT=words[tab, o, g][:, t * P : (t + 1) * P].bitcast(FP8X4),
+                    lhsT_scale=scales[tab][k0:P, g * SPAN + t * P : g * SPAN + (t + 1) * P],
+                    rhs=h_codes[o][:].bitcast(FP8X4),
+                    rhs_scale=h_scales[o][:],
+                    start=(o == 0),
+                    stop=(o == PASSES - 1),
+                )
+
+        for g in range(GROUPS):
+            gather_words("x", 0, g)
+        deal_scales("x", gather_scales("x"))
+        quantize_h(0)
+        for g in range(GROUPS):
+            products("x", 0, g)
+        deal_scales("e", gather_scales("e"))
+        quantize_h(1)
+        gates = {}
+        for g in range(GROUPS):
+            gather_words("x", 1, g)
+            products("x", 1, g)
+            for t in range(PACK):
+                gates[g, t] = keep.tile([P, J], F32, name="gate%d%d" % (g, t))
+                nc.scalar.activation(out=gates[g, t][:], in_=acc["x", g, t][:], func=GELU)
+        for o in range(PASSES):
+            for g in range(GROUPS):
+                gather_words("e", o, g)
+                products("e", o, g)
+
+        out_scales = keep.tile([P, GROUPS, J], U8, name="out_scales", align_bytes=64)
+        rounded_out = {}
+        for g in range(GROUPS):
+            for h in range(HALVES):
+                cols = slice(h * HALF, (h + 1) * HALF)
+                res = keep.tile([P, PACK, HALF], F32, name="res%d%d" % (g, h))
+                for t in range(PACK):
+                    nc.vector.tensor_tensor(res[:, t, :], acc["e", g, t][:, cols], gates[g, t][:, cols], MULT)
+                nc.sync.dma_start(out=out_0[g * SPAN : (g + 1) * SPAN, cols].rearrange("(p t) j -> p t j", t=PACK), in_=res[:])
+                rounded_out[g, h] = keep.tile([P, HALF, PACK], BF16, name="rounded_out%d%d" % (g, h), align_bytes=64)
+                interleave(rounded_out[g, h], res)
+        for g in range(GROUPS):
+            for h in range(HALVES):
+                cols = slice(h * HALF, (h + 1) * HALF)
+                codes = keep.tile([P, HALF], U32, name="out_codes%d%d" % (g, h), align_bytes=64)
+                nc.vector.quantize_mx(out=codes[:].bitcast(FP8X4), scales=out_scales[:, g, cols],
+                                      in_=rounded_out[g, h][:].rearrange("p j t -> p (j t)"))
+                nc.sync.dma_start(out=out_1[g][:, cols, :].rearrange("p n t -> p (n t)").bitcast(I32), in_=codes[:].bitcast(I32))
+        for q in range(QUADS):
+            queue = nc.scalar if q % 2 else nc.sync
+            queue.dma_start(out=out_2[:, 4 * q : 4 * q + 4, :].rearrange("g r j -> r g j").bitcast(I32),
+                            in_=out_scales[32 * q : 32 * q + 4, :, :].bitcast(I32))

@@ -48,7 +48,7 @@ def tile_picked_zdejag_gelu_po_kernel(tc, x_words, x_scales, e_words, e_scales, 
         def load_scales(tab):
             for q in range(QUADS):
                 r0 = 32 * q + scale_row0[tab]
-                nc.sync.dma_start(out=scale_win[tab][r0 : r0 + 4 * PASSES, :].bitcast(I32),
+                nc.gpsimd.dma_start(out=scale_win[tab][r0 : r0 + 4 * PASSES, :].bitcast(I32),
                                   in_=scale_src[tab][:, 4 * q : 4 * q + 4, :].bitcast(I32))
 
         h_raw = {}
@@ -57,12 +57,12 @@ def tile_picked_zdejag_gelu_po_kernel(tc, x_words, x_scales, e_words, e_scales, 
             h_raw[o] = keep.tile([P, PACK, J], F32, name="h_raw%d" % o)
             nc.sync.dma_start(out=h_raw[o][:], in_=hT[o * SPAN : (o + 1) * SPAN, :].rearrange("(p t) j -> p t j", t=PACK))
 
+        load_scales("x")
+        load_scales("e")
         load_words("x", 0)
         nc.sync.dma_start(offsets[:], offs)
-        load_scales("x")
         load_h(0)
         load_h(1)
-        load_scales("e")
         load_words("x", 1)
         load_words("e", 0)
         load_words("e", 1)
@@ -141,7 +141,9 @@ def tile_picked_zdejag_gelu_po_kernel(tc, x_words, x_scales, e_words, e_scales, 
                 res = keep.tile([P, PACK, HALF], F32, name="res%d%d" % (g, h))
                 for t in range(PACK):
                     nc.vector.tensor_tensor(res[:, t, :], acc["e", g, t][:, cols], gates[g, t][:, cols], MULT)
-                nc.sync.dma_start(out=out_0[g * SPAN : (g + 1) * SPAN, cols].rearrange("(p t) j -> p t j", t=PACK), in_=res[:])
+                rows = out_0[g * SPAN : (g + 1) * SPAN, cols].rearrange("(p t) j -> p t j", t=PACK)
+                for ts in ([slice(0, 2), slice(2, 4)] if (g, h) == (0, 0) else [slice(0, 4)]):
+                    nc.sync.dma_start(out=rows[:, ts, :], in_=res[:, ts, :])
                 rounded_out[g, h] = keep.tile([P, HALF, PACK], BF16, name="rounded_out%d%d" % (g, h), align_bytes=64)
                 interleave(rounded_out[g, h], res)
         for g in range(GROUPS):

@@ -32,7 +32,6 @@ def tile_picked_zdejag_gelu_po_kernel(tc, x_words, x_scales, e_words, e_scales, 
         psum = ctx.enter_context(tc.psum_pool(name="psum", bufs=1))
 
         offsets = keep.tile([P, S // 16], U16, name="offsets")
-        scale_row0 = {"x": 0, "e": PASSES * 4}
         word_src = {"x": x_words, "e": e_words}
         scale_src = {"x": x_scales, "e": e_scales}
         word_win, scale_win = {}, {}
@@ -46,10 +45,8 @@ def tile_picked_zdejag_gelu_po_kernel(tc, x_words, x_scales, e_words, e_scales, 
             word_win[tab, o] = win
 
         def load_scales(tab):
-            for q in range(QUADS):
-                r0 = 32 * q + scale_row0[tab]
-                nc.gpsimd.dma_start(out=scale_win[tab][r0 : r0 + 4 * PASSES, :].bitcast(I32),
-                                  in_=scale_src[tab][:, 4 * q : 4 * q + 4, :].bitcast(I32))
+            for o in range(PASSES):
+                nc.sync.dma_start(out=scale_win[tab][4 * o : P : 8, :].bitcast(I32), in_=scale_src[tab][o].bitcast(I32))
 
         h_raw = {}
 
@@ -57,18 +54,16 @@ def tile_picked_zdejag_gelu_po_kernel(tc, x_words, x_scales, e_words, e_scales, 
             h_raw[o] = keep.tile([P, PACK, J], F32, name="h_raw%d" % o)
             nc.sync.dma_start(out=h_raw[o][:], in_=hT[o * SPAN : (o + 1) * SPAN, :].rearrange("(p t) j -> p t j", t=PACK))
 
+        load_h(0)
+        nc.sync.dma_start(offsets[:], offs)
         load_scales("x")
         load_scales("e")
         load_words("x", 0)
-        nc.sync.dma_start(offsets[:], offs)
-        load_h(0)
         load_h(1)
         load_words("x", 1)
-        load_words("e", 0)
-        load_words("e", 1)
 
         def interleave(dst, src):
-            nc.scalar.copy(out=dst[:].rearrange("p (c i) t -> p c t i", i=4), in_=src[:].rearrange("p t (c i) -> p c t i", i=4))
+            nc.scalar.copy(out=dst.rearrange("p (c i) t -> p c t i", i=4), in_=src.rearrange("p t (c i) -> p c t i", i=4))
 
         words, scales, h_codes, h_scales = {}, {}, {}, {}
 
@@ -87,11 +82,16 @@ def tile_picked_zdejag_gelu_po_kernel(tc, x_words, x_scales, e_words, e_scales, 
             dealt = keep.tile([P, S], U8, name="scales_" + tab, align_bytes=64)
             nc.vector.tensor_copy(dealt[:].rearrange("p (g t s) -> p g t s", g=GROUPS, t=PACK),
                                   picked[:].rearrange("p (g s t) -> p g t s", g=GROUPS, t=PACK))
-            scales[tab] = dealt
+            planes = keep.tile([P, S], U8, name="planes_" + tab, align_bytes=64)
+            nc.vector.tensor_copy(planes[:].bitcast(I32), dealt[:].bitcast(I32))
+            for o in range(PASSES):
+                for r in range(1, 4):
+                    nc.sync.dma_start(out=planes[4 * o + r : P : 32, :].bitcast(I32), in_=dealt[4 * o + 8 * r : P : 32, :].bitcast(I32))
+            scales[tab] = planes
 
         def quantize_h(o):
             rounded = keep.tile([P, J, PACK], BF16, name="h_rounded%d" % o, align_bytes=64)
-            interleave(rounded, h_raw[o])
+            interleave(rounded[:], h_raw[o][:])
             h_codes[o] = keep.tile([P, J], U32, name="h_codes%d" % o, align_bytes=64)
             h_scales[o] = keep.tile([P, J], U8, name="h_scales%d" % o, align_bytes=64)
             nc.vector.quantize_mx(out=h_codes[o][:].bitcast(FP8X4), scales=h_scales[o][:], in_=rounded[:].rearrange("p j t -> p (j t)"))
@@ -102,7 +102,7 @@ def tile_picked_zdejag_gelu_po_kernel(tc, x_words, x_scales, e_words, e_scales, 
             for t in range(PACK):
                 if o == 0:
                     acc[tab, g, t] = psum.tile([P, J], F32, name="acc_%s%d%d" % (tab, g, t), tag="bank%d%d" % (g, t))
-                k0 = scale_row0[tab] + 4 * o
+                k0 = 4 * o
                 nc.tensor.matmul_mx(
                     out=acc[tab, g, t][:],
                     lhsT=words[tab, o, g][:, t * P : (t + 1) * P].bitcast(FP8X4),
@@ -113,14 +113,16 @@ def tile_picked_zdejag_gelu_po_kernel(tc, x_words, x_scales, e_words, e_scales, 
                     stop=(o == PASSES - 1),
                 )
 
+        deal_scales("x", gather_scales("x"))
+        load_words("e", 0)
+        quantize_h(0)
+        deal_scales("e", gather_scales("e"))
+        load_words("e", 1)
         for g in range(GROUPS):
             gather_words("x", 0, g)
-        deal_scales("x", gather_scales("x"))
-        quantize_h(0)
+        quantize_h(1)
         for g in range(GROUPS):
             products("x", 0, g)
-        deal_scales("e", gather_scales("e"))
-        quantize_h(1)
         gates = {}
         for g in range(GROUPS):
             gather_words("x", 1, g)
@@ -134,25 +136,29 @@ def tile_picked_zdejag_gelu_po_kernel(tc, x_words, x_scales, e_words, e_scales, 
                 products("e", o, g)
 
         out_scales = keep.tile([P, GROUPS, J], U8, name="out_scales", align_bytes=64)
+        pieces = {0: [(0, 256), (256, 512)], 1: [(0, 256), (256, 384), (384, 512)]}
         rounded_out = {}
         for g in range(GROUPS):
-            for h in range(HALVES):
-                cols = slice(h * HALF, (h + 1) * HALF)
-                res = keep.tile([P, PACK, HALF], F32, name="res%d%d" % (g, h))
+            res = keep.tile([P, PACK, J], F32, name="res%d" % g)
+            rows = out_0[g * SPAN : (g + 1) * SPAN, :].rearrange("(p t) j -> p t j", t=PACK)
+            for a, b in pieces[g]:
                 for t in range(PACK):
-                    nc.vector.tensor_tensor(res[:, t, :], acc["e", g, t][:, cols], gates[g, t][:, cols], MULT)
-                rows = out_0[g * SPAN : (g + 1) * SPAN, cols].rearrange("(p t) j -> p t j", t=PACK)
-                for ts in ([slice(0, 2), slice(2, 4)] if (g, h) == (0, 0) else [slice(0, 4)]):
-                    nc.sync.dma_start(out=rows[:, ts, :], in_=res[:, ts, :])
-                rounded_out[g, h] = keep.tile([P, HALF, PACK], BF16, name="rounded_out%d%d" % (g, h), align_bytes=64)
-                interleave(rounded_out[g, h], res)
+                    nc.vector.tensor_tensor(res[:, t, a:b], acc["e", g, t][:, a:b], gates[g, t][:, a:b], MULT)
+                    if (g, a) == (0, 0) and t % 2:
+                        nc.sync.dma_start(out=rows[:, t - 1 : t + 1, a:b], in_=res[:, t - 1 : t + 1, a:b])
+                if b % HALF == 0 and (g, a) != (0, 0):
+                    nc.sync.dma_start(out=rows[:, :, b - HALF : b], in_=res[:, :, b - HALF : b])
+                rounded_out[g, a] = keep.tile([P, b - a, PACK], BF16, name="rounded_out%d_%d" % (g, a), align_bytes=64)
+                interleave(rounded_out[g, a][:], res[:, :, a:b])
         for g in range(GROUPS):
-            for h in range(HALVES):
-                cols = slice(h * HALF, (h + 1) * HALF)
-                codes = keep.tile([P, HALF], U32, name="out_codes%d%d" % (g, h), align_bytes=64)
-                nc.vector.quantize_mx(out=codes[:].bitcast(FP8X4), scales=out_scales[:, g, cols],
-                                      in_=rounded_out[g, h][:].rearrange("p j t -> p (j t)"))
-                nc.sync.dma_start(out=out_1[g][:, cols, :].rearrange("p n t -> p (n t)").bitcast(I32), in_=codes[:].bitcast(I32))
+            codes = keep.tile([P, J], U32, name="out_codes%d" % g, align_bytes=64)
+            stored = 0
+            for a, b in pieces[g]:
+                nc.vector.quantize_mx(out=codes[:, a:b].bitcast(FP8X4), scales=out_scales[:, g, a:b],
+                                      in_=rounded_out[g, a][:].rearrange("p j t -> p (j t)"))
+                if b > HALF:
+                    nc.sync.dma_start(out=out_1[g][:, stored:b, :].rearrange("p n t -> p (n t)").bitcast(I32), in_=codes[:, stored:b].bitcast(I32))
+                    stored = b
         for q in range(QUADS):
             queue = nc.scalar if q % 2 else nc.sync
             queue.dma_start(out=out_2[:, 4 * q : 4 * q + 4, :].rearrange("g r j -> r g j").bitcast(I32),

@@ -39,28 +39,32 @@ def tile_picked_zdejag_gelu_po_kernel(tc, x_words, x_scales, e_words, e_scales, 
             scale_win[tab] = keep.tile([P, T], U8, name="scale_win_" + tab, align_bytes=64)
             nc.vector.memset(scale_win[tab][:].bitcast(I32), 0)
 
-        def load_words(tab, o):
-            win = keep.tile([P, T], U32, name="word_win_%s%d" % (tab, o), align_bytes=64)
-            nc.sync.dma_start(out=win[:].bitcast(I32), in_=word_src[tab][o].rearrange("p n t -> p (n t)").bitcast(I32))
-            word_win[tab, o] = win
+        for tab in "xe":
+            for o in range(PASSES):
+                word_win[tab, o] = keep.tile([P, T], U32, name="word_win_%s%d" % (tab, o), align_bytes=64)
+
+        def load_words(tab, o, cols=slice(0, T)):
+            nc.sync.dma_start(out=word_win[tab, o][:, cols].bitcast(I32),
+                              in_=word_src[tab][o][:, cols, :].rearrange("p n t -> p (n t)").bitcast(I32))
 
         def load_scales(tab):
             for o in range(PASSES):
                 nc.sync.dma_start(out=scale_win[tab][4 * o : P : 8, :].bitcast(I32), in_=scale_src[tab][o].bitcast(I32))
 
-        h_raw = {}
+        h_raw = [keep.tile([P, PACK, J], F32, name="h_raw%d" % o) for o in range(PASSES)]
 
-        def load_h(o):
-            h_raw[o] = keep.tile([P, PACK, J], F32, name="h_raw%d" % o)
-            nc.sync.dma_start(out=h_raw[o][:], in_=hT[o * SPAN : (o + 1) * SPAN, :].rearrange("(p t) j -> p t j", t=PACK))
+        def load_h(o, ts):
+            rows = hT[o * SPAN : (o + 1) * SPAN, :].rearrange("(p t) j -> p t j", t=PACK)
+            nc.sync.dma_start(out=h_raw[o][:, ts, :], in_=rows[:, ts, :])
 
-        load_h(0)
+        load_h(0, slice(0, 2))
         nc.sync.dma_start(offsets[:], offs)
         load_scales("x")
+        load_h(0, slice(2, 4))
         load_scales("e")
         load_words("x", 0)
-        load_h(1)
-        load_words("x", 1)
+        load_h(1, slice(0, 4))
+        load_words("x", 1, slice(0, T // 2))
 
         def interleave(dst, src):
             nc.scalar.copy(out=dst.rearrange("p (c i) t -> p c t i", i=4), in_=src.rearrange("p t (c i) -> p c t i", i=4))
@@ -84,9 +88,8 @@ def tile_picked_zdejag_gelu_po_kernel(tc, x_words, x_scales, e_words, e_scales, 
                                   picked[:].rearrange("p (g s t) -> p g t s", g=GROUPS, t=PACK))
             planes = keep.tile([P, S], U8, name="planes_" + tab, align_bytes=64)
             nc.vector.tensor_copy(planes[:].bitcast(I32), dealt[:].bitcast(I32))
-            for o in range(PASSES):
-                for r in range(1, 4):
-                    nc.sync.dma_start(out=planes[4 * o + r : P : 32, :].bitcast(I32), in_=dealt[4 * o + 8 * r : P : 32, :].bitcast(I32))
+            for r in range(1, 4):
+                nc.sync.dma_start(out=planes[r : r + 4 * 25 + 1 : 4, :].bitcast(I32), in_=dealt[8 * r : 8 * r + 4 * 25 + 1 : 4, :].bitcast(I32))
             scales[tab] = planes
 
         def quantize_h(o):
@@ -114,10 +117,11 @@ def tile_picked_zdejag_gelu_po_kernel(tc, x_words, x_scales, e_words, e_scales, 
                 )
 
         deal_scales("x", gather_scales("x"))
+        load_words("x", 1, slice(T // 2, T))
         load_words("e", 0)
-        quantize_h(0)
         deal_scales("e", gather_scales("e"))
         load_words("e", 1)
+        quantize_h(0)
         for g in range(GROUPS):
             gather_words("x", 0, g)
         quantize_h(1)

@@ -140,29 +140,50 @@ def tile_picked_zdejag_gelu_po_kernel(tc, x_words, x_scales, e_words, e_scales, 
                 products("e", o, g)
 
         out_scales = keep.tile([P, GROUPS, J], U8, name="out_scales", align_bytes=64)
-        pieces = {0: [(0, 256), (256, 512)], 1: [(0, 256), (256, 384), (384, 512)]}
+        halves = [slice(0, HALF), slice(HALF, J)]
         rounded_out = {}
+
+        def round_out(g, h, res, on_vector):
+            rounded_out[g, h] = keep.tile([P, HALF, PACK], BF16, name="rounded_out%d_%d" % (g, h), align_bytes=64)
+            dst = rounded_out[g, h][:].rearrange("p (c i) t -> p c t i", i=4)
+            src = res[:, :, halves[h]].rearrange("p t (c i) -> p c t i", i=4)
+            if on_vector:
+                nc.vector.tensor_copy(dst, src)
+            else:
+                nc.scalar.copy(out=dst, in_=src)
+
+        codes = [keep.tile([P, J], U32, name="out_codes%d" % g, align_bytes=64) for g in range(GROUPS)]
+
+        def quantize_out(g, h):
+            nc.vector.quantize_mx(out=codes[g][:, halves[h]].bitcast(FP8X4), scales=out_scales[:, g, halves[h]],
+                                  in_=rounded_out[g, h][:].rearrange("p j t -> p (j t)"))
+
+        def store_codes(g, cols):
+            nc.sync.dma_start(out=out_1[g][:, cols, :].rearrange("p n t -> p (n t)").bitcast(I32), in_=codes[g][:, cols].bitcast(I32))
+
         for g in range(GROUPS):
             res = keep.tile([P, PACK, J], F32, name="res%d" % g)
             rows = out_0[g * SPAN : (g + 1) * SPAN, :].rearrange("(p t) j -> p t j", t=PACK)
-            for a, b in pieces[g]:
-                for t in range(PACK):
-                    nc.vector.tensor_tensor(res[:, t, a:b], acc["e", g, t][:, a:b], gates[g, t][:, a:b], MULT)
-                    if (g, a) == (0, 0) and t % 2:
-                        nc.sync.dma_start(out=rows[:, t - 1 : t + 1, a:b], in_=res[:, t - 1 : t + 1, a:b])
-                if b % HALF == 0 and (g, a) != (0, 0):
-                    nc.sync.dma_start(out=rows[:, :, b - HALF : b], in_=res[:, :, b - HALF : b])
-                rounded_out[g, a] = keep.tile([P, b - a, PACK], BF16, name="rounded_out%d_%d" % (g, a), align_bytes=64)
-                interleave(rounded_out[g, a][:], res[:, :, a:b])
-        for g in range(GROUPS):
-            codes = keep.tile([P, J], U32, name="out_codes%d" % g, align_bytes=64)
-            stored = 0
-            for a, b in pieces[g]:
-                nc.vector.quantize_mx(out=codes[:, a:b].bitcast(FP8X4), scales=out_scales[:, g, a:b],
-                                      in_=rounded_out[g, a][:].rearrange("p j t -> p (j t)"))
-                if b > HALF:
-                    nc.sync.dma_start(out=out_1[g][:, stored:b, :].rearrange("p n t -> p (n t)").bitcast(I32), in_=codes[:, stored:b].bitcast(I32))
-                    stored = b
+            for t in (0, 1):
+                nc.vector.tensor_tensor(res[:, t, :], acc["e", g, t][:], gates[g, t][:], MULT)
+                if g == 0:
+                    nc.sync.dma_start(out=rows[:, t, :], in_=res[:, t, :])
+            if g == 1:
+                nc.sync.dma_start(out=rows[:, 0:2, :], in_=res[:, 0:2, :])
+            for h in range(HALVES):
+                for t in (2, 3):
+                    nc.vector.tensor_tensor(res[:, t, halves[h]], acc["e", g, t][:, halves[h]], gates[g, t][:, halves[h]], MULT)
+                if h == 1:
+                    nc.sync.dma_start(out=rows[:, 2:4, :], in_=res[:, 2:4, :])
+                if (g, h) != (1, 1):
+                    round_out(g, h, res, False)
+        quantize_out(0, 0)
+        quantize_out(0, 1)
+        store_codes(0, slice(0, J))
+        round_out(1, 1, res, True)
+        quantize_out(1, 0)
+        quantize_out(1, 1)
+        store_codes(1, slice(0, J))
         for q in range(QUADS):
             queue = nc.scalar if q % 2 else nc.sync
             queue.dma_start(out=out_2[:, 4 * q : 4 * q + 4, :].rearrange("g r j -> r g j").bitcast(I32),

@@ -161,29 +161,43 @@ def tile_picked_zdejag_gelu_po_kernel(tc, x_words, x_scales, e_words, e_scales, 
         def store_codes(g, cols):
             nc.sync.dma_start(out=out_1[g][:, cols, :].rearrange("p n t -> p (n t)").bitcast(I32), in_=codes[g][:, cols].bitcast(I32))
 
-        for g in range(GROUPS):
-            res = keep.tile([P, PACK, J], F32, name="res%d" % g)
-            rows = out_0[g * SPAN : (g + 1) * SPAN, :].rearrange("(p t) j -> p t j", t=PACK)
-            for t in (0, 1):
-                nc.vector.tensor_tensor(res[:, t, :], acc["e", g, t][:], gates[g, t][:], MULT)
-                if g == 0:
-                    nc.sync.dma_start(out=rows[:, t, :], in_=res[:, t, :])
-            if g == 1:
-                nc.sync.dma_start(out=rows[:, 0:2, :], in_=res[:, 0:2, :])
-            for h in range(HALVES):
-                for t in (2, 3):
-                    nc.vector.tensor_tensor(res[:, t, halves[h]], acc["e", g, t][:, halves[h]], gates[g, t][:, halves[h]], MULT)
-                if h == 1:
-                    nc.sync.dma_start(out=rows[:, 2:4, :], in_=res[:, 2:4, :])
-                if (g, h) != (1, 1):
-                    round_out(g, h, res, False)
+        results = [keep.tile([P, PACK, J], F32, name="res%d" % g) for g in range(GROUPS)]
+        rows = [out_0[g * SPAN : (g + 1) * SPAN, :].rearrange("(p t) j -> p t j", t=PACK) for g in range(GROUPS)]
+
+        def multiply(g, t, cols):
+            nc.vector.tensor_tensor(results[g][:, t, cols], acc["e", g, t][:, cols], gates[g, t][:, cols], MULT)
+
+        def store_rows(g, ts):
+            nc.sync.dma_start(out=rows[g][:, ts, :], in_=results[g][:, ts, :])
+
+        values = [keep.tile([P, HALF], F32, name="values%d" % h) for h in range(HALVES)]
+        for h in range(HALVES):
+            nc.scalar.copy(out=values[h][:], in_=acc["e", 0, 0][:, halves[h]])
+            nc.gpsimd.tensor_tensor(results[0][:, 0, halves[h]], values[h][:], gates[0, 0][:, halves[h]], MULT)
+        for t in (1, 2):
+            multiply(0, t, slice(0, J))
+            store_rows(0, slice(t, t + 1))
+        store_rows(0, slice(0, 1))
+        for h in range(HALVES):
+            multiply(0, 3, halves[h])
+            round_out(0, h, results[0], False)
+        store_rows(0, slice(3, 4))
+        for t in (0, 1):
+            multiply(1, t, slice(0, J))
+        store_rows(1, slice(0, 2))
+        for h in range(HALVES):
+            for t in (2, 3):
+                multiply(1, t, halves[h])
+        store_rows(1, slice(2, 4))
+        round_out(1, 0, results[1], False)
+        res = results[1]
         quantize_out(0, 0)
         quantize_out(0, 1)
         store_codes(0, slice(0, J))
         round_out(1, 1, res, True)
-        quantize_out(1, 0)
-        quantize_out(1, 1)
-        store_codes(1, slice(0, J))
+        for h in range(HALVES):
+            quantize_out(1, h)
+            store_codes(1, halves[h])
         for q in range(QUADS):
             queue = nc.scalar if q % 2 else nc.sync
             queue.dma_start(out=out_2[:, 4 * q : 4 * q + 4, :].rearrange("g r j -> r g j").bitcast(I32),

@@ -48,8 +48,7 @@ def tile_picked_zdejag_gelu_po_kernel(tc, x_words, x_scales, e_words, e_scales, 
                               in_=word_src[tab][o][:, cols, :].rearrange("p n t -> p (n t)").bitcast(I32))
 
         def load_scales(tab):
-            for o in range(PASSES):
-                nc.sync.dma_start(out=scale_win[tab][4 * o : P : 8, :].bitcast(I32), in_=scale_src[tab][o].bitcast(I32))
+            nc.sync.dma_start(out=scale_win[tab][0:P:4, :].bitcast(I32), in_=scale_src[tab].rearrange("o q n -> q o n").bitcast(I32))
 
         h_raw = [keep.tile([P, PACK, J], F32, name="h_raw%d" % o) for o in range(PASSES)]
 
@@ -57,14 +56,13 @@ def tile_picked_zdejag_gelu_po_kernel(tc, x_words, x_scales, e_words, e_scales, 
             rows = hT[o * SPAN : (o + 1) * SPAN, :].rearrange("(p t) j -> p t j", t=PACK)
             nc.sync.dma_start(out=h_raw[o][:, ts, :], in_=rows[:, ts, :])
 
-        load_h(0, slice(0, 2))
+        load_h(0, slice(0, 4))
         nc.sync.dma_start(offsets[:], offs)
         load_scales("x")
-        load_h(0, slice(2, 4))
         load_scales("e")
         load_words("x", 0)
         load_h(1, slice(0, 4))
-        load_words("x", 1, slice(0, T // 2))
+        load_words("x", 1)
 
         def interleave(dst, src):
             nc.scalar.copy(out=dst.rearrange("p (c i) t -> p c t i", i=4), in_=src.rearrange("p t (c i) -> p c t i", i=4))
@@ -117,7 +115,6 @@ def tile_picked_zdejag_gelu_po_kernel(tc, x_words, x_scales, e_words, e_scales, 
                 )
 
         deal_scales("x", gather_scales("x"))
-        load_words("x", 1, slice(T // 2, T))
         load_words("e", 0)
         deal_scales("e", gather_scales("e"))
         load_words("e", 1)
@@ -125,11 +122,10 @@ def tile_picked_zdejag_gelu_po_kernel(tc, x_words, x_scales, e_words, e_scales, 
         for g in range(GROUPS):
             gather_words("x", 0, g)
         quantize_h(1)
-        for g in range(GROUPS):
-            products("x", 0, g)
         gates = {}
         for g in range(GROUPS):
             gather_words("x", 1, g)
+            products("x", 0, g)
             products("x", 1, g)
             for t in range(PACK):
                 gates[g, t] = keep.tile([P, J], F32, name="gate%d%d" % (g, t))
@@ -167,24 +163,30 @@ def tile_picked_zdejag_gelu_po_kernel(tc, x_words, x_scales, e_words, e_scales, 
         def multiply(g, t, cols):
             nc.vector.tensor_tensor(results[g][:, t, cols], acc["e", g, t][:, cols], gates[g, t][:, cols], MULT)
 
-        def store_rows(g, ts):
-            nc.sync.dma_start(out=rows[g][:, ts, :], in_=results[g][:, ts, :])
+        def store_rows(g, ts, cols=slice(0, J)):
+            nc.sync.dma_start(out=rows[g][:, ts, cols], in_=results[g][:, ts, cols])
 
-        values = [keep.tile([P, HALF], F32, name="values%d" % h) for h in range(HALVES)]
+        def multiply_aside(g, t, h):
+            values = keep.tile([P, HALF], F32, name="values%d%d%d" % (g, t, h))
+            nc.scalar.copy(out=values[:], in_=acc["e", g, t][:, halves[h]])
+            nc.gpsimd.tensor_tensor(results[g][:, t, halves[h]], values[:], gates[g, t][:, halves[h]], MULT)
+
+        for g in range(GROUPS):
+            for h in range(HALVES):
+                multiply_aside(g, 0, h)
         for h in range(HALVES):
-            nc.scalar.copy(out=values[h][:], in_=acc["e", 0, 0][:, halves[h]])
-            nc.gpsimd.tensor_tensor(results[0][:, 0, halves[h]], values[h][:], gates[0, 0][:, halves[h]], MULT)
-        for t in (1, 2):
-            multiply(0, t, slice(0, J))
-            store_rows(0, slice(t, t + 1))
+            multiply(0, 1, halves[h])
+            store_rows(0, slice(1, 2), halves[h])
+        multiply(0, 2, slice(0, J))
+        store_rows(0, slice(2, 3))
         store_rows(0, slice(0, 1))
         for h in range(HALVES):
             multiply(0, 3, halves[h])
             round_out(0, h, results[0], False)
         store_rows(0, slice(3, 4))
-        for t in (0, 1):
-            multiply(1, t, slice(0, J))
-        store_rows(1, slice(0, 2))
+        multiply(1, 1, slice(0, J))
+        store_rows(1, slice(1, 2))
+        store_rows(1, slice(0, 1))
         for h in range(HALVES):
             for t in (2, 3):
                 multiply(1, t, halves[h])

@@ -48,7 +48,8 @@ def tile_picked_zdejag_gelu_po_kernel(tc, x_words, x_scales, e_words, e_scales, 
                               in_=word_src[tab][o][:, cols, :].rearrange("p n t -> p (n t)").bitcast(I32))
 
         def load_scales(tab):
-            nc.sync.dma_start(out=scale_win[tab][0:P:4, :].bitcast(I32), in_=scale_src[tab].rearrange("o q n -> q o n").bitcast(I32))
+            for o in range(PASSES):
+                nc.sync.dma_start(out=scale_win[tab][4 * o : P : 8, :].bitcast(I32), in_=scale_src[tab][o].bitcast(I32))
 
         h_raw = [keep.tile([P, PACK, J], F32, name="h_raw%d" % o) for o in range(PASSES)]
 
@@ -56,13 +57,14 @@ def tile_picked_zdejag_gelu_po_kernel(tc, x_words, x_scales, e_words, e_scales, 
             rows = hT[o * SPAN : (o + 1) * SPAN, :].rearrange("(p t) j -> p t j", t=PACK)
             nc.sync.dma_start(out=h_raw[o][:, ts, :], in_=rows[:, ts, :])
 
-        load_h(0, slice(0, 4))
+        load_h(0, slice(0, 2))
         nc.sync.dma_start(offsets[:], offs)
         load_scales("x")
+        load_h(0, slice(2, 4))
         load_scales("e")
         load_words("x", 0)
         load_h(1, slice(0, 4))
-        load_words("x", 1)
+        load_words("x", 1, slice(0, T // 2))
 
         def interleave(dst, src):
             nc.scalar.copy(out=dst.rearrange("p (c i) t -> p c t i", i=4), in_=src.rearrange("p t (c i) -> p c t i", i=4))
@@ -115,6 +117,7 @@ def tile_picked_zdejag_gelu_po_kernel(tc, x_words, x_scales, e_words, e_scales, 
                 )
 
         deal_scales("x", gather_scales("x"))
+        load_words("x", 1, slice(T // 2, T))
         load_words("e", 0)
         deal_scales("e", gather_scales("e"))
         load_words("e", 1)
@@ -122,10 +125,11 @@ def tile_picked_zdejag_gelu_po_kernel(tc, x_words, x_scales, e_words, e_scales, 
         for g in range(GROUPS):
             gather_words("x", 0, g)
         quantize_h(1)
+        for g in range(GROUPS):
+            products("x", 0, g)
         gates = {}
         for g in range(GROUPS):
             gather_words("x", 1, g)
-            products("x", 0, g)
             products("x", 1, g)
             for t in range(PACK):
                 gates[g, t] = keep.tile([P, J], F32, name="gate%d%d" % (g, t))
@@ -139,10 +143,13 @@ def tile_picked_zdejag_gelu_po_kernel(tc, x_words, x_scales, e_words, e_scales, 
         halves = [slice(0, HALF), slice(HALF, J)]
         rounded_out = {}
 
-        def round_out(g, h, res, on_vector):
-            rounded_out[g, h] = keep.tile([P, HALF, PACK], BF16, name="rounded_out%d_%d" % (g, h), align_bytes=64)
-            dst = rounded_out[g, h][:].rearrange("p (c i) t -> p c t i", i=4)
-            src = res[:, :, halves[h]].rearrange("p t (c i) -> p c t i", i=4)
+        for g in range(GROUPS):
+            for h in range(HALVES):
+                rounded_out[g, h] = keep.tile([P, HALF, PACK], BF16, name="rounded_out%d_%d" % (g, h), align_bytes=64)
+
+        def round_out(g, h, res, on_vector, a=0, b=HALF):
+            dst = rounded_out[g, h][:, a:b, :].rearrange("p (c i) t -> p c t i", i=4)
+            src = res[:, :, h * HALF + a : h * HALF + b].rearrange("p t (c i) -> p c t i", i=4)
             if on_vector:
                 nc.vector.tensor_copy(dst, src)
             else:
@@ -177,9 +184,10 @@ def tile_picked_zdejag_gelu_po_kernel(tc, x_words, x_scales, e_words, e_scales, 
         for h in range(HALVES):
             multiply(0, 1, halves[h])
             store_rows(0, slice(1, 2), halves[h])
+        store_rows(0, slice(0, 1), halves[0])
         multiply(0, 2, slice(0, J))
         store_rows(0, slice(2, 3))
-        store_rows(0, slice(0, 1))
+        store_rows(0, slice(0, 1), halves[1])
         for h in range(HALVES):
             multiply(0, 3, halves[h])
             round_out(0, h, results[0], False)
@@ -190,14 +198,15 @@ def tile_picked_zdejag_gelu_po_kernel(tc, x_words, x_scales, e_words, e_scales, 
         for h in range(HALVES):
             for t in (2, 3):
                 multiply(1, t, halves[h])
+            if h == 0:
+                round_out(1, 0, results[1], False, 0, 192)
         store_rows(1, slice(2, 4))
-        round_out(1, 0, results[1], False)
-        res = results[1]
         quantize_out(0, 0)
+        round_out(1, 1, results[1], True)
+        round_out(1, 0, results[1], True, 192, HALF)
         quantize_out(0, 1)
         store_codes(0, slice(0, J))
-        round_out(1, 1, res, True)
-        for h in range(HALVES):
+        for h in (1, 0):
             quantize_out(1, h)
             store_codes(1, halves[h])
         for q in range(QUADS):

@@ -102,7 +102,7 @@ def tile_picked_zdejag_gelu_po_kernel(tc, x_words, x_scales, e_words, e_scales, 
         acc = {}
 
         def products(tab, o, g):
-            for t in range(PACK):
+            for t in (3, 0, 1, 2):
                 if o == 0:
                     acc[tab, g, t] = psum.tile([P, J], F32, name="acc_%s%d%d" % (tab, g, t), tag="bank%d%d" % (g, t))
                 k0 = 4 * o
@@ -131,7 +131,7 @@ def tile_picked_zdejag_gelu_po_kernel(tc, x_words, x_scales, e_words, e_scales, 
         for g in range(GROUPS):
             gather_words("x", 1, g)
             products("x", 1, g)
-            for t in range(PACK):
+            for t in (3, 0, 1, 2):
                 gates[g, t] = keep.tile([P, J], F32, name="gate%d%d" % (g, t))
                 nc.scalar.activation(out=gates[g, t][:], in_=acc["x", g, t][:], func=GELU)
         for o in range(PASSES):
@@ -180,26 +180,20 @@ def tile_picked_zdejag_gelu_po_kernel(tc, x_words, x_scales, e_words, e_scales, 
 
         for g in range(GROUPS):
             for h in range(HALVES):
-                multiply_aside(g, 0, h)
+                multiply_aside(g, 3, h)
+        for t in (0, 1):
+            multiply(0, t, slice(0, J))
+            store_rows(0, slice(t, t + 1))
         for h in range(HALVES):
-            multiply(0, 1, halves[h])
-            store_rows(0, slice(1, 2), halves[h])
-        store_rows(0, slice(0, 1), halves[0])
-        multiply(0, 2, slice(0, J))
-        store_rows(0, slice(2, 3))
-        store_rows(0, slice(0, 1), halves[1])
-        for h in range(HALVES):
-            multiply(0, 3, halves[h])
+            multiply(0, 2, halves[h])
             round_out(0, h, results[0], False)
-        store_rows(0, slice(3, 4))
-        multiply(1, 1, slice(0, J))
-        store_rows(1, slice(1, 2))
-        store_rows(1, slice(0, 1))
-        for h in range(HALVES):
-            for t in (2, 3):
-                multiply(1, t, halves[h])
-            if h == 0:
-                round_out(1, 0, results[1], False, 0, 192)
+        store_rows(0, slice(2, 4))
+        for t in (0, 1):
+            multiply(1, t, slice(0, J))
+        store_rows(1, slice(0, 2))
+        multiply(1, 2, halves[0])
+        round_out(1, 0, results[1], False, 0, 192)
+        multiply(1, 2, halves[1])
         store_rows(1, slice(2, 4))
         quantize_out(0, 0)
         round_out(1, 1, results[1], True)
@@ -208,7 +202,7 @@ def tile_picked_zdejag_gelu_po_kernel(tc, x_words, x_scales, e_words, e_scales, 
         store_codes(0, slice(0, J))
         for h in (1, 0):
             quantize_out(1, h)
-            store_codes(1, halves[h])
+        store_codes(1, slice(0, J))
         for q in range(QUADS):
             queue = nc.scalar if q % 2 else nc.sync
             queue.dma_start(out=out_2[:, 4 * q : 4 * q + 4, :].rearrange("g r j -> r g j").bitcast(I32),

@@ -23,6 +23,7 @@ GROUPS = S // SPAN
 QUADS = 4
 HALVES = 2
 HALF = J // HALVES
+E_FIRST = 1024
 
 
 def tile_picked_zdejag_gelu_po_kernel(tc, x_words, x_scales, e_words, e_scales, hT, offs, out_0, out_1, out_2):
@@ -64,12 +65,13 @@ def tile_picked_zdejag_gelu_po_kernel(tc, x_words, x_scales, e_words, e_scales, 
         load_scales("e")
         load_words("x", 0)
         load_h(1, slice(0, 4))
-        load_words("x", 1, slice(0, T // 2))
+        load_words("x", 1)
+        load_words("e", 0, slice(0, E_FIRST))
 
         def interleave(dst, src):
             nc.scalar.copy(out=dst.rearrange("p (c i) t -> p c t i", i=4), in_=src.rearrange("p t (c i) -> p c t i", i=4))
 
-        words, scales, h_codes, h_scales = {}, {}, {}, {}
+        words, h_codes, h_scales = {}, {}, {}
 
         def gather_words(tab, o, g):
             picked = keep.tile([P, SPAN], U32, name="words_%s%d%d" % (tab, o, g), align_bytes=64)
@@ -77,20 +79,21 @@ def tile_picked_zdejag_gelu_po_kernel(tc, x_words, x_scales, e_words, e_scales, 
             nc.vector.tensor_copy(picked[:].rearrange("p (t s) -> p s t", t=PACK), word_win[tab, o][:].indirect(offsets[:, cols]))
             words[tab, o, g] = picked
 
-        def gather_scales(tab):
+        dealt = keep.tile([P, 2 * S], U8, name="dealt", align_bytes=64)
+        planes = keep.tile([P, 2 * S], U8, name="planes", align_bytes=64)
+
+        def pick_scales(tab):
+            cols = slice("xe".index(tab) * S, ("xe".index(tab) + 1) * S)
             picked = keep.tile([P, S], U8, name="picked_scales_" + tab, align_bytes=64)
             nc.vector.tensor_copy(picked[:], scale_win[tab][:].indirect(offsets[:]))
-            return picked
-
-        def deal_scales(tab, picked):
-            dealt = keep.tile([P, S], U8, name="scales_" + tab, align_bytes=64)
-            nc.vector.tensor_copy(dealt[:].rearrange("p (g t s) -> p g t s", g=GROUPS, t=PACK),
+            nc.vector.tensor_copy(dealt[:, cols].rearrange("p (g t s) -> p g t s", g=GROUPS, t=PACK),
                                   picked[:].rearrange("p (g s t) -> p g t s", g=GROUPS, t=PACK))
-            planes = keep.tile([P, S], U8, name="planes_" + tab, align_bytes=64)
-            nc.vector.tensor_copy(planes[:].bitcast(I32), dealt[:].bitcast(I32))
-            for r in range(1, 4):
-                nc.sync.dma_start(out=planes[r : r + 4 * 25 + 1 : 4, :].bitcast(I32), in_=dealt[8 * r : 8 * r + 4 * 25 + 1 : 4, :].bitcast(I32))
-            scales[tab] = planes
+            nc.vector.tensor_copy(planes[:, cols].bitcast(I32), dealt[:, cols].bitcast(I32))
+
+        def move_scales():
+            for o in range(PASSES):
+                for r in range(1, 4):
+                    nc.sync.dma_start(out=planes[4 * o + r : P : 32, :].bitcast(I32), in_=dealt[4 * o + 8 * r : P : 32, :].bitcast(I32))
 
         def quantize_h(o):
             rounded = keep.tile([P, J, PACK], BF16, name="h_rounded%d" % o, align_bytes=64)
@@ -101,43 +104,41 @@ def tile_picked_zdejag_gelu_po_kernel(tc, x_words, x_scales, e_words, e_scales, 
 
         acc = {}
 
-        def products(tab, o, g):
-            for t in (3, 0, 1, 2):
-                if o == 0:
-                    acc[tab, g, t] = psum.tile([P, J], F32, name="acc_%s%d%d" % (tab, g, t), tag="bank%d%d" % (g, t))
-                k0 = 4 * o
-                nc.tensor.matmul_mx(
-                    out=acc[tab, g, t][:],
-                    lhsT=words[tab, o, g][:, t * P : (t + 1) * P].bitcast(FP8X4),
-                    lhsT_scale=scales[tab][k0:P, g * SPAN + t * P : g * SPAN + (t + 1) * P],
-                    rhs=h_codes[o][:].bitcast(FP8X4),
-                    rhs_scale=h_scales[o][:],
-                    start=(o == 0),
-                    stop=(o == PASSES - 1),
-                )
+        def product(tab, o, g, t):
+            if o == 0:
+                acc[tab, g, t] = psum.tile([P, J], F32, name="acc_%s%d%d" % (tab, g, t), tag="bank%d%d" % (g, t))
+            c0 = "xe".index(tab) * S + g * SPAN + t * P
+            nc.tensor.matmul_mx(
+                out=acc[tab, g, t][:],
+                lhsT=words[tab, o, g][:, t * P : (t + 1) * P].bitcast(FP8X4),
+                lhsT_scale=planes[4 * o : P, c0 : c0 + P],
+                rhs=h_codes[o][:].bitcast(FP8X4),
+                rhs_scale=h_scales[o][:],
+                start=(o == 0),
+                stop=(o == PASSES - 1),
+            )
 
-        deal_scales("x", gather_scales("x"))
-        load_words("x", 1, slice(T // 2, T))
-        load_words("e", 0)
-        deal_scales("e", gather_scales("e"))
+        pick_scales("x")
+        pick_scales("e")
+        move_scales()
+        load_words("e", 0, slice(E_FIRST, T))
         load_words("e", 1)
-        quantize_h(0)
-        for g in range(GROUPS):
-            gather_words("x", 0, g)
-        quantize_h(1)
-        for g in range(GROUPS):
-            products("x", 0, g)
+        for o in range(PASSES):
+            quantize_h(o)
+            for g in range(GROUPS):
+                gather_words("x", o, g)
         gates = {}
         for g in range(GROUPS):
-            gather_words("x", 1, g)
-            products("x", 1, g)
             for t in (3, 0, 1, 2):
+                for o in range(PASSES):
+                    product("x", o, g, t)
                 gates[g, t] = keep.tile([P, J], F32, name="gate%d%d" % (g, t))
                 nc.scalar.activation(out=gates[g, t][:], in_=acc["x", g, t][:], func=GELU)
         for o in range(PASSES):
             for g in range(GROUPS):
                 gather_words("e", o, g)
-                products("e", o, g)
+                for t in (3, 0, 1, 2):
+                    product("e", o, g, t)
 
         out_scales = keep.tile([P, GROUPS, J], U8, name="out_scales", align_bytes=64)
         halves = [slice(0, HALF), slice(HALF, J)]

@@ -23,7 +23,6 @@ GROUPS = S // SPAN
 QUADS = 4
 HALVES = 2
 HALF = J // HALVES
-E_FIRST = 1024
 
 
 def tile_picked_zdejag_gelu_po_kernel(tc, x_words, x_scales, e_words, e_scales, hT, offs, out_0, out_1, out_2):
@@ -64,9 +63,8 @@ def tile_picked_zdejag_gelu_po_kernel(tc, x_words, x_scales, e_words, e_scales, 
         load_h(0, slice(2, 4))
         load_scales("e")
         load_words("x", 0)
-        load_h(1, slice(0, 4))
         load_words("x", 1)
-        load_words("e", 0, slice(0, E_FIRST))
+        load_h(1, slice(0, 4))
 
         def interleave(dst, src):
             nc.scalar.copy(out=dst.rearrange("p (c i) t -> p c t i", i=4), in_=src.rearrange("p t (c i) -> p c t i", i=4))
@@ -91,8 +89,8 @@ def tile_picked_zdejag_gelu_po_kernel(tc, x_words, x_scales, e_words, e_scales, 
             nc.vector.tensor_copy(planes[:, cols].bitcast(I32), dealt[:, cols].bitcast(I32))
 
         def move_scales():
-            for o in range(PASSES):
-                for r in range(1, 4):
+            for r in range(1, 4):
+                for o in range(PASSES):
                     nc.sync.dma_start(out=planes[4 * o + r : P : 32, :].bitcast(I32), in_=dealt[4 * o + 8 * r : P : 32, :].bitcast(I32))
 
         def quantize_h(o):
@@ -121,17 +119,20 @@ def tile_picked_zdejag_gelu_po_kernel(tc, x_words, x_scales, e_words, e_scales, 
         pick_scales("x")
         pick_scales("e")
         move_scales()
-        load_words("e", 0, slice(E_FIRST, T))
+        load_words("e", 0)
         load_words("e", 1)
+        quantize_h(0)
         for o in range(PASSES):
-            quantize_h(o)
             for g in range(GROUPS):
                 gather_words("x", o, g)
+        quantize_h(1)
+        for g in range(GROUPS):
+            for t in (3, 0, 1, 2):
+                product("x", 0, g, t)
         gates = {}
         for g in range(GROUPS):
             for t in (3, 0, 1, 2):
-                for o in range(PASSES):
-                    product("x", o, g, t)
+                product("x", 1, g, t)
                 gates[g, t] = keep.tile([P, J], F32, name="gate%d%d" % (g, t))
                 nc.scalar.activation(out=gates[g, t][:], in_=acc["x", g, t][:], func=GELU)
         for o in range(PASSES):

@@ -37,7 +37,7 @@ def tile_picked_zdejag_gelu_po_kernel(tc, x_words, x_scales, e_words, e_scales, 
         word_win, scale_win = {}, {}
         for tab in "xe":
             scale_win[tab] = keep.tile([P, T], U8, name="scale_win_" + tab, align_bytes=64)
-            nc.vector.memset(scale_win[tab][:].bitcast(I32), 0)
+            (nc.vector if tab == "x" else nc.gpsimd).memset(scale_win[tab][:].bitcast(I32), 0)
 
         for tab in "xe":
             for o in range(PASSES):
@@ -57,10 +57,9 @@ def tile_picked_zdejag_gelu_po_kernel(tc, x_words, x_scales, e_words, e_scales, 
             rows = hT[o * SPAN : (o + 1) * SPAN, :].rearrange("(p t) j -> p t j", t=PACK)
             nc.sync.dma_start(out=h_raw[o][:, ts, :], in_=rows[:, ts, :])
 
-        load_h(0, slice(0, 2))
+        load_h(0, slice(0, 4))
         nc.sync.dma_start(offsets[:], offs)
         load_scales("x")
-        load_h(0, slice(2, 4))
         load_scales("e")
         load_words("x", 0)
         load_words("x", 1)
@@ -80,6 +79,8 @@ def tile_picked_zdejag_gelu_po_kernel(tc, x_words, x_scales, e_words, e_scales, 
         dealt = keep.tile([P, 2 * S], U8, name="dealt", align_bytes=64)
         planes = keep.tile([P, 2 * S], U8, name="planes", align_bytes=64)
 
+        second = {tab: keep.tile([P, S], U8, name="second_" + tab, align_bytes=64) for tab in "xe"}
+
         def pick_scales(tab):
             cols = slice("xe".index(tab) * S, ("xe".index(tab) + 1) * S)
             picked = keep.tile([P, S], U8, name="picked_scales_" + tab, align_bytes=64)
@@ -87,11 +88,10 @@ def tile_picked_zdejag_gelu_po_kernel(tc, x_words, x_scales, e_words, e_scales, 
             nc.vector.tensor_copy(dealt[:, cols].rearrange("p (g t s) -> p g t s", g=GROUPS, t=PACK),
                                   picked[:].rearrange("p (g s t) -> p g t s", g=GROUPS, t=PACK))
             nc.vector.tensor_copy(planes[:, cols].bitcast(I32), dealt[:, cols].bitcast(I32))
+            nc.vector.tensor_copy(second[tab][:].bitcast(I32), dealt[:, cols].bitcast(I32))
 
-        def move_scales():
-            for r in range(1, 4):
-                for o in range(PASSES):
-                    nc.sync.dma_start(out=planes[4 * o + r : P : 32, :].bitcast(I32), in_=dealt[4 * o + 8 * r : P : 32, :].bitcast(I32))
+        def move_scales(o, r, plane, cols):
+            nc.sync.dma_start(out=plane[4 * o + r : P : 32, :].bitcast(I32), in_=dealt[4 * o + 8 * r : P : 32, cols].bitcast(I32))
 
         def quantize_h(o):
             rounded = keep.tile([P, J, PACK], BF16, name="h_rounded%d" % o, align_bytes=64)
@@ -105,11 +105,12 @@ def tile_picked_zdejag_gelu_po_kernel(tc, x_words, x_scales, e_words, e_scales, 
         def product(tab, o, g, t):
             if o == 0:
                 acc[tab, g, t] = psum.tile([P, J], F32, name="acc_%s%d%d" % (tab, g, t), tag="bank%d%d" % (g, t))
-            c0 = "xe".index(tab) * S + g * SPAN + t * P
+            c0 = g * SPAN + t * P
+            plane = second[tab][4:P, c0 : c0 + P] if o else planes[:, "xe".index(tab) * S + c0 : "xe".index(tab) * S + c0 + P]
             nc.tensor.matmul_mx(
                 out=acc[tab, g, t][:],
                 lhsT=words[tab, o, g][:, t * P : (t + 1) * P].bitcast(FP8X4),
-                lhsT_scale=planes[4 * o : P, c0 : c0 + P],
+                lhsT_scale=plane,
                 rhs=h_codes[o][:].bitcast(FP8X4),
                 rhs_scale=h_scales[o][:],
                 start=(o == 0),
@@ -118,9 +119,13 @@ def tile_picked_zdejag_gelu_po_kernel(tc, x_words, x_scales, e_words, e_scales, 
 
         pick_scales("x")
         pick_scales("e")
-        move_scales()
+        for r in range(1, 4):
+            move_scales(0, r, planes, slice(0, 2 * S))
+            move_scales(1, r, second["x"], slice(0, S))
         load_words("e", 0)
         load_words("e", 1)
+        for r in range(1, 4):
+            move_scales(1, r, second["e"], slice(S, 2 * S))
         quantize_h(0)
         for o in range(PASSES):
             for g in range(GROUPS):

@@ -211,6 +211,5 @@ def tile_picked_zdejag_gelu_po_kernel(tc, x_words, x_scales, e_words, e_scales, 
             quantize_out(1, h)
         store_codes(1, slice(0, J))
         for q in range(QUADS):
-            queue = nc.scalar if q % 2 else nc.sync
-            queue.dma_start(out=out_2[:, 4 * q : 4 * q + 4, :].rearrange("g r j -> r g j").bitcast(I32),
-                            in_=out_scales[32 * q : 32 * q + 4, :, :].bitcast(I32))
+            nc.sync.dma_start(out=out_2[:, 4 * q : 4 * q + 4, :].rearrange("g r j -> r g j").bitcast(I32),
+                              in_=out_scales[32 * q : 32 * q + 4, :, :].bitcast(I32))

@@ -210,6 +210,6 @@ def tile_picked_zdejag_gelu_po_kernel(tc, x_words, x_scales, e_words, e_scales, 
         for h in (1, 0):
             quantize_out(1, h)
         store_codes(1, slice(0, J))
-        for q in range(QUADS):
-            nc.sync.dma_start(out=out_2[:, 4 * q : 4 * q + 4, :].rearrange("g r j -> r g j").bitcast(I32),
-                              in_=out_scales[32 * q : 32 * q + 4, :, :].bitcast(I32))
+        for r in range(QUADS):
+            nc.sync.dma_start(out=out_2[:, r : 16 : 4, :].rearrange("g q j -> q g j").bitcast(I32),
+                              in_=out_scales[r : P : 32, :, :].bitcast(I32))

from contextlib import ExitStack

import concourse.mybir as mybir

K, T, S, J = 1024, 4096, 1024, 512
FLOPS = 2 * 2 * K * S * J

F32 = mybir.dt.float32
BF16 = mybir.dt.bfloat16
I32 = mybir.dt.int32
U32 = mybir.dt.uint32
U16 = mybir.dt.uint16
U8 = mybir.dt.uint8
FP8X4 = mybir.dt.float8_e4m3fn_x4
GELU = mybir.ActivationFunctionType.Gelu_apprx_tanh
MULT = mybir.AluOpType.mult

P = 128
PACK = 4
SPAN = P * PACK
PASSES = K // SPAN
GROUPS = S // SPAN
QUADS = 4
HALVES = 2
HALF = J // HALVES


def tile_picked_zdejag_gelu_po_kernel(tc, x_words, x_scales, e_words, e_scales, hT, offs, out_0, out_1, out_2):
    nc = tc.nc
    with ExitStack() as ctx:
        keep = ctx.enter_context(tc.tile_pool(name="keep", bufs=1))
        psum = ctx.enter_context(tc.psum_pool(name="psum", bufs=1))

        offsets = keep.tile([P, S // 16], U16, name="offsets")
        word_src = {"x": x_words, "e": e_words}
        scale_src = {"x": x_scales, "e": e_scales}
        word_win, scale_win = {}, {}
        for tab in "xe":
            scale_win[tab] = keep.tile([P, T], U8, name="scale_win_" + tab, align_bytes=64)
            (nc.vector if tab == "x" else nc.gpsimd).memset(scale_win[tab][:].bitcast(I32), 0)

        for tab in "xe":
            for o in range(PASSES):
                word_win[tab, o] = keep.tile([P, T], U32, name="word_win_%s%d" % (tab, o), align_bytes=64)

        def load_words(tab, o, cols=slice(0, T)):
            nc.sync.dma_start(out=word_win[tab, o][:, cols].bitcast(I32),
                              in_=word_src[tab][o][:, cols, :].rearrange("p n t -> p (n t)").bitcast(I32))

        def load_scales(tab):
            for o in range(PASSES):
                nc.sync.dma_start(out=scale_win[tab][4 * o : P : 8, :].bitcast(I32), in_=scale_src[tab][o].bitcast(I32))

        h_raw = [keep.tile([P, PACK, J], F32, name="h_raw%d" % o) for o in range(PASSES)]

        def load_h(o, ts):
            rows = hT[o * SPAN : (o + 1) * SPAN, :].rearrange("(p t) j -> p t j", t=PACK)
            nc.sync.dma_start(out=h_raw[o][:, ts, :], in_=rows[:, ts, :])

        load_h(0, slice(0, 4))
        nc.sync.dma_start(offsets[:], offs)
        load_scales("x")
        load_scales("e")
        load_words("x", 0)
        load_words("x", 1)
        load_h(1, slice(0, 4))

        def interleave(dst, src):
            nc.scalar.copy(out=dst.rearrange("p (c i) t -> p c t i", i=4), in_=src.rearrange("p t (c i) -> p c t i", i=4))

        words, h_codes, h_scales = {}, {}, {}

        def gather_words(tab, o, g):
            picked = keep.tile([P, SPAN], U32, name="words_%s%d%d" % (tab, o, g), align_bytes=64)
            cols = slice(g * SPAN // 16, (g + 1) * SPAN // 16)
            nc.vector.tensor_copy(picked[:].rearrange("p (t s) -> p s t", t=PACK), word_win[tab, o][:].indirect(offsets[:, cols]))
            words[tab, o, g] = picked

        dealt = keep.tile([P, 2 * S], U8, name="dealt", align_bytes=64)
        planes = keep.tile([P, 2 * S], U8, name="planes", align_bytes=64)

        second = {tab: keep.tile([P, S], U8, name="second_" + tab, align_bytes=64) for tab in "xe"}

        def pick_scales(tab):
            cols = slice("xe".index(tab) * S, ("xe".index(tab) + 1) * S)
            picked = keep.tile([P, S], U8, name="picked_scales_" + tab, align_bytes=64)
            nc.vector.tensor_copy(picked[:], scale_win[tab][:].indirect(offsets[:]))
            nc.vector.tensor_copy(dealt[:, cols].rearrange("p (g t s) -> p g t s", g=GROUPS, t=PACK),
                                  picked[:].rearrange("p (g s t) -> p g t s", g=GROUPS, t=PACK))
            nc.vector.tensor_copy(planes[:, cols].bitcast(I32), dealt[:, cols].bitcast(I32))
            nc.vector.tensor_copy(second[tab][:].bitcast(I32), dealt[:, cols].bitcast(I32))

        def move_scales(o, r, plane, cols):
            nc.sync.dma_start(out=plane[4 * o + r : P : 32, :].bitcast(I32), in_=dealt[4 * o + 8 * r : P : 32, cols].bitcast(I32))

        def quantize_h(o):
            rounded = keep.tile([P, J, PACK], BF16, name="h_rounded%d" % o, align_bytes=64)
            interleave(rounded[:], h_raw[o][:])
            h_codes[o] = keep.tile([P, J], U32, name="h_codes%d" % o, align_bytes=64)
            h_scales[o] = keep.tile([P, J], U8, name="h_scales%d" % o, align_bytes=64)
            nc.vector.quantize_mx(out=h_codes[o][:].bitcast(FP8X4), scales=h_scales[o][:], in_=rounded[:].rearrange("p j t -> p (j t)"))

        acc = {}

        def product(tab, o, g, t):
            if o == 0:
                acc[tab, g, t] = psum.tile([P, J], F32, name="acc_%s%d%d" % (tab, g, t), tag="bank%d%d" % (g, t))
            c0 = g * SPAN + t * P
            plane = second[tab][4:P, c0 : c0 + P] if o else planes[:, "xe".index(tab) * S + c0 : "xe".index(tab) * S + c0 + P]
            nc.tensor.matmul_mx(
                out=acc[tab, g, t][:],
                lhsT=words[tab, o, g][:, t * P : (t + 1) * P].bitcast(FP8X4),
                lhsT_scale=plane,
                rhs=h_codes[o][:].bitcast(FP8X4),
                rhs_scale=h_scales[o][:],
                start=(o == 0),
                stop=(o == PASSES - 1),
            )

        pick_scales("x")
        pick_scales("e")
        for r in range(1, 4):
            move_scales(0, r, planes, slice(0, 2 * S))
            move_scales(1, r, second["x"], slice(0, S))
        load_words("e", 0)
        load_words("e", 1)
        for r in range(1, 4):
            move_scales(1, r, second["e"], slice(S, 2 * S))
        quantize_h(0)
        for o in range(PASSES):
            for g in range(GROUPS):
                gather_words("x", o, g)
        quantize_h(1)
        for g in range(GROUPS):
            for t in (3, 0, 1, 2):
                product("x", 0, g, t)
        gates = {}
        for g in range(GROUPS):
            for t in (3, 0, 1, 2):
                product("x", 1, g, t)
                gates[g, t] = keep.tile([P, J], F32, name="gate%d%d" % (g, t))
                nc.scalar.activation(out=gates[g, t][:], in_=acc["x", g, t][:], func=GELU)
        for o in range(PASSES):
            for g in range(GROUPS):
                gather_words("e", o, g)
                for t in (3, 0, 1, 2):
                    product("e", o, g, t)

        out_scales = keep.tile([P, GROUPS, J], U8, name="out_scales", align_bytes=64)
        halves = [slice(0, HALF), slice(HALF, J)]
        rounded_out = {}

        for g in range(GROUPS):
            for h in range(HALVES):
                rounded_out[g, h] = keep.tile([P, HALF, PACK], BF16, name="rounded_out%d_%d" % (g, h), align_bytes=64)

        def round_out(g, h, res, on_vector, a=0, b=HALF):
            dst = rounded_out[g, h][:, a:b, :].rearrange("p (c i) t -> p c t i", i=4)
            src = res[:, :, h * HALF + a : h * HALF + b].rearrange("p t (c i) -> p c t i", i=4)
            if on_vector:
                nc.vector.tensor_copy(dst, src)
            else:
                nc.scalar.copy(out=dst, in_=src)

        codes = [keep.tile([P, J], U32, name="out_codes%d" % g, align_bytes=64) for g in range(GROUPS)]

        def quantize_out(g, h):
            nc.vector.quantize_mx(out=codes[g][:, halves[h]].bitcast(FP8X4), scales=out_scales[:, g, halves[h]],
                                  in_=rounded_out[g, h][:].rearrange("p j t -> p (j t)"))

        def store_codes(g, cols):
            nc.sync.dma_start(out=out_1[g][:, cols, :].rearrange("p n t -> p (n t)").bitcast(I32), in_=codes[g][:, cols].bitcast(I32))

        results = [keep.tile([P, PACK, J], F32, name="res%d" % g) for g in range(GROUPS)]
        rows = [out_0[g * SPAN : (g + 1) * SPAN, :].rearrange("(p t) j -> p t j", t=PACK) for g in range(GROUPS)]

        def multiply(g, t, cols):
            nc.vector.tensor_tensor(results[g][:, t, cols], acc["e", g, t][:, cols], gates[g, t][:, cols], MULT)

        def store_rows(g, ts, cols=slice(0, J)):
            nc.sync.dma_start(out=rows[g][:, ts, cols], in_=results[g][:, ts, cols])

        def multiply_aside(g, t, h):
            values = keep.tile([P, HALF], F32, name="values%d%d%d" % (g, t, h))
            nc.scalar.copy(out=values[:], in_=acc["e", g, t][:, halves[h]])
            nc.gpsimd.tensor_tensor(results[g][:, t, halves[h]], values[:], gates[g, t][:, halves[h]], MULT)

        for g in range(GROUPS):
            for h in range(HALVES):
                multiply_aside(g, 3, h)
        for t in (0, 1):
            multiply(0, t, slice(0, J))
            store_rows(0, slice(t, t + 1))
        for h in range(HALVES):
            multiply(0, 2, halves[h])
            round_out(0, h, results[0], False)
        store_rows(0, slice(2, 4))
        for t in (0, 1):
            multiply(1, t, slice(0, J))
        store_rows(1, slice(0, 2))
        multiply(1, 2, halves[0])
        round_out(1, 0, results[1], False, 0, 192)
        multiply(1, 2, halves[1])
        store_rows(1, slice(2, 4))
        quantize_out(0, 0)
        round_out(1, 1, results[1], True)
        round_out(1, 0, results[1], True, 192, HALF)
        quantize_out(0, 1)
        store_codes(0, slice(0, J))
        for h in (1, 0):
            quantize_out(1, h)
        store_codes(1, slice(0, J))
        for r in range(QUADS):
            nc.sync.dma_start(out=out_2[:, r : 16 : 4, :].rearrange("g q j -> q g j").bitcast(I32),
                              in_=out_scales[r : P : 32, :, :].bitcast(I32))
